import numpy as np
import ml_dtypes


def mxq(x, axis, fmt="e4m3"):
    dtype, down = {"e4m3": (ml_dtypes.float8_e4m3fn, 7), "e5m2": (ml_dtypes.float8_e5m2, 14)}[fmt]
    v = np.moveaxis(np.asarray(x, np.float32).astype(ml_dtypes.bfloat16).astype(np.float64), axis, -1)
    blocks = v.reshape(v.shape[:-1] + (-1, 32))
    amax = np.abs(blocks).max(-1, keepdims=True)
    byte = np.maximum(np.where(amax > 0, np.frexp(amax)[1] - 1 + 127, 0) - down, 1)
    scale = np.exp2(byte - 127.0)
    codes = (blocks / scale).astype(np.float32).astype(dtype).astype(np.float64)
    return np.moveaxis((codes * scale).reshape(v.shape), -1, axis)


WIDE = False


def mx_kscale(k):
    if not WIDE:
        return np.ones(k)
    levels = np.array([10, -10, 5, -5, 0])
    if k % 512:
        return np.exp2(np.random.permutation(np.resize(levels, k // 32))).repeat(32)
    a = np.empty((k // 512, 16))
    for p in range(k // 512):
        a[p, :8] = np.random.permutation(np.resize(levels, 8))
        for g in range(8):
            far = levels[np.abs(levels - a[p, g]) >= 10]
            a[p, g + 8] = far[np.random.randint(len(far))]
    return np.exp2(a.ravel()).repeat(32)


def f64(x):
    return np.asarray(x).astype(np.float64)


def striped(idx):
    return np.tile(idx.reshape(-1, 16).T, (8, 1)).astype(np.uint16)


def unstriped(offs):
    return offs[:16].T.reshape(-1).astype(np.int64)


def striped8(idx):
    return np.concatenate([x.reshape(-1, 16).T for x in idx]).astype(np.uint16)


def runs(offs, k):
    lists = np.stack([offs[16 * r : 16 * r + 16].T.reshape(-1) for r in range(8)]).astype(np.int64)
    return lists[np.arange(k) % 512 // 64]


def pack_weight(w):
    k, n = w.shape
    w = f64(np.asarray(w, np.float32).astype(ml_dtypes.bfloat16)).reshape(k // 32, 32, n)
    amax = np.abs(w).max(1)
    byte = np.clip(np.where(amax > 0, np.frexp(amax)[1] - 1 + 127 - 7, 1), 1, 254)
    scaled = (w * np.exp2(127.0 - byte)[:, None, :]).reshape(k, n).astype(np.float32)
    words = np.ascontiguousarray(scaled.reshape(k // 512, 128, 4, n).transpose(0, 1, 3, 2)).astype(ml_dtypes.float8_e4m3fn).view(np.uint8)
    return words, np.ascontiguousarray(byte.astype(np.uint8).reshape(k // 512, 16, n))


def unpack_weight(words, scales):
    g, p, n, _ = words.shape
    vals = np.ascontiguousarray(words).view(ml_dtypes.float8_e4m3fn).astype(np.float64) * np.repeat(np.exp2(scales.astype(np.float64) - 127.0), 8, axis=1)[..., None]
    return vals.transpose(0, 1, 3, 2).reshape(g * 512, n)


K, T, S, V, H, C = 512, 2048, 512, 256, 512, 512


def setup_inputs():
    n = np.random.standard_normal
    s = mx_kscale(K)[:, None]
    packed_xT = pack_weight(n((K, T)) * s)
    perm = np.stack([np.random.permutation(S) for _ in range(8)])
    perm2 = np.stack([np.random.permutation(S) for _ in range(8)])
    return {
        "x_words": packed_xT[0],
        "x_scales": packed_xT[1],
        "w1": (n((K, H)) / np.sqrt(K) / s).astype(np.float32),
        "gs": (np.random.uniform(0.5, 1.5, (K, 1)) / s).astype(np.float32),
        "offs": striped(np.random.permutation(T)[:S]),
        "la": striped8(perm[:, :V]),
        "lb": striped8(perm[:, V:]),
        "ma": striped8(perm2[:, :V]),
        "mb": striped8(perm2[:, V:]),
        "cand": striped(np.random.permutation(T)[:C]),
    }


def reference(x_words, x_scales, w1, gs, offs, la, lb, ma, mb, cand):
    x_cand = unpack_weight(x_words, x_scales)[:, unstriped(cand)]
    xq = unpack_weight(x_words, x_scales)[:, unstriped(offs)]
    y = mxq(f64(w1), 0, "e4m3").T @ xq
    x1 = np.maximum(y[np.arange(H)[:, None], runs(la, H)], y[np.arange(H)[:, None], runs(lb, H)])
    n1 = np.minimum(y[np.arange(H)[:, None], runs(la, H)], y[np.arange(H)[:, None], runs(lb, H)])
    h0 = np.zeros((H, S))
    h0[np.arange(H)[:, None], runs(la, H)] = n1
    h = h0.copy()
    h[np.arange(H)[:, None], runs(lb, H)] = x1
    x2 = np.maximum(h[np.arange(H)[:, None], runs(ma, H)], h[np.arange(H)[:, None], runs(mb, H)])
    n2 = np.minimum(h[np.arange(H)[:, None], runs(ma, H)], h[np.arange(H)[:, None], runs(mb, H)])
    h2 = np.zeros((H, S))
    h2[np.arange(H)[:, None], runs(ma, H)] = n2
    h3 = h2.copy()
    h3[np.arange(H)[:, None], runs(mb, H)] = x2
    z = f64(gs) * h3
    return 0.0625 * ((x_cand.T @ mxq(z, 0, "e4m3")))

@@ -1,0 +1,168 @@
+from contextlib import ExitStack
+
+import concourse.mybir as mybir
+
+K, T, S, V, H, C = 512, 2048, 512, 256, 512, 512
+FLOPS = 2 * K * H * S + 2 * H * C * S
+
+F32 = mybir.dt.float32
+BF16 = mybir.dt.bfloat16
+I32 = mybir.dt.int32
+U32 = mybir.dt.uint32
+U16 = mybir.dt.uint16
+U8 = mybir.dt.uint8
+FP8X4 = mybir.dt.float8_e4m3fn_x4
+ALU = mybir.AluOpType
+COPY = mybir.ActivationFunctionType.Copy
+
+P = 128
+PACK = 4
+HALF = 256
+OUT_SCALE = 0.0625
+
+
+def tile_picked_bitonic2_none_p_kernel(tc, x_words, x_scales, w1, gs, offs, la, lb, ma, mb, cand, out):
+    nc = tc.nc
+    with ExitStack() as ctx:
+        keep = ctx.enter_context(tc.tile_pool(name="keep", bufs=1))
+        ring = ctx.enter_context(tc.tile_pool(name="ring", bufs=3))
+        psum = ctx.enter_context(tc.psum_pool(name="psum", bufs=8))
+
+        def load_list(name, src):
+            tile = keep.tile(list(src.shape), U16, name=name)
+            nc.sync.dma_start(tile[:], src)
+            return tile
+
+        table_words = keep.tile([P, T], I32, name="table_words", align_bytes=64)
+        table_scales = keep.tile([P, T], U8, name="table_scales", align_bytes=64)
+        nc.vector.memset(table_scales[:].bitcast(I32), 0)
+
+        w_rows = w1.rearrange("(p j) c -> p j c", j=PACK)
+        w_raw = [keep.tile([P, PACK, HALF], F32, name="w_raw%d" % i) for i in range(2)]
+        nc.sync.dma_start(w_raw[0][:], w_rows[:, :, 0:HALF])
+        for q in range(4):
+            nc.sync.dma_start(
+                table_scales[32 * q : 32 * q + 4, :].bitcast(I32),
+                x_scales[0, 4 * q : 4 * q + 4, :].bitcast(I32),
+            )
+        nc.sync.dma_start(w_raw[1][:], w_rows[:, :, HALF : 2 * HALF])
+        offs_t = load_list("offs_t", offs)
+        nc.sync.dma_start(table_words[:], x_words[0].rearrange("p n t -> p (n t)").bitcast(I32))
+        cand_t = load_list("cand_t", cand)
+        la_t = load_list("la_t", la)
+        lb_t = load_list("lb_t", lb)
+        ma_t = load_list("ma_t", ma)
+        mb_t = load_list("mb_t", mb)
+        gains = keep.tile([P, PACK], F32, name="gains")
+        nc.sync.dma_start(gains[:], gs.rearrange("(p t) o -> p (t o)", t=PACK))
+
+        tok_scales = keep.tile([P, S], U8, name="tok_scales", align_bytes=64)
+        cand_scales = keep.tile([P, C], U8, name="cand_scales", align_bytes=64)
+        tok_words = keep.tile([P, S], U32, name="tok_words", align_bytes=64)
+        cand_words = keep.tile([P, C], U32, name="cand_words", align_bytes=64)
+        nc.vector.tensor_copy(tok_scales[:], table_scales[:].indirect(offs_t[:]))
+        nc.vector.tensor_copy(cand_scales[:], table_scales[:].indirect(cand_t[:]))
+
+        w_bf = keep.tile([P, PACK, P, PACK], BF16, name="w_bf", align_bytes=64)
+        per = HALF // PACK
+        for i in range(2):
+            nc.scalar.copy(
+                w_bf[:, :, i * per : (i + 1) * per, :].rearrange("p t m j -> p m t j"),
+                w_raw[i][:].rearrange("p j (m t) -> p m t j", t=PACK),
+            )
+        w_words = keep.tile([P, H], U32, name="w_words", align_bytes=64)
+        w_scales = keep.tile([P, H], U8, name="w_scales", align_bytes=64)
+        nc.vector.quantize_mx(
+            out=w_words[:].bitcast(FP8X4),
+            scales=w_scales[:],
+            in_=w_bf[:].rearrange("p t m j -> p (t m j)"),
+        )
+
+        nc.vector.tensor_copy(tok_words[:], table_words[:].bitcast(U32).indirect(offs_t[:]))
+        nc.vector.tensor_copy(cand_words[:], table_words[:].bitcast(U32).indirect(cand_t[:]))
+
+        order = (2, 0, 1, 3)
+        y = {}
+        for t in order:
+            acc = psum.tile([P, S], F32, name="acc")
+            cols = slice(t * P, (t + 1) * P)
+            nc.tensor.matmul_mx(
+                out=acc[:],
+                lhsT=w_words[:, cols].bitcast(FP8X4),
+                lhsT_scale=w_scales[:, cols],
+                rhs=tok_words[:].bitcast(FP8X4),
+                rhs_scale=tok_scales[:],
+                start=True,
+                stop=True,
+            )
+            y[t] = keep.tile([P, S], F32, name="y%d" % t)
+            nc.scalar.copy(y[t][:], acc[:])
+
+        h = {t: keep.tile([P, S], F32, name="h%d" % t) for t in order}
+        steps = [(0, t) for t in order] + [(1, t) for t in order]
+        lists = ((la_t, lb_t), (ma_t, mb_t))
+        z_bf = keep.tile([P, S, PACK], BF16, name="z_bf", align_bytes=64)
+
+        def fetch(step, side):
+            stage, t = step
+            window = y[t] if stage == 0 else h[t]
+            got = ring.tile([P, V], F32, name="got%d" % side)
+            nc.vector.tensor_copy(got[:], window[:].indirect(lists[stage][side][:]))
+            return got
+
+        a = fetch(steps[0], 0)
+        b = fetch(steps[0], 1)
+        for n, (stage, t) in enumerate(steps):
+            more = n + 1 < len(steps)
+            lo = ring.tile([P, V], F32, name="lo")
+            hi = ring.tile([P, V], F32, name="hi")
+            nc.vector.tensor_tensor(lo[:], a[:], b[:], ALU.min)
+            nc.vector.tensor_tensor(hi[:], a[:], b[:], ALU.max)
+            if stage == 0:
+                target = h[t]
+            else:
+                target = ring.tile([P, S], F32, name="h3")
+            if more:
+                a = fetch(steps[n + 1], 0)
+            nc.vector.tensor_copy(target[:].indirect(lists[stage][0][:]), lo[:])
+            if more:
+                b = fetch(steps[n + 1], 1)
+            nc.vector.tensor_copy(target[:].indirect(lists[stage][1][:]), hi[:])
+            if stage == 1 and more:
+                nc.scalar.activation(z_bf[:, :, t], target[:], COPY, scale=gains[:, t : t + 1])
+
+        gain = gains[:, t : t + 1]
+        for quarter in range(4):
+            cols = slice(quarter * P, (quarter + 1) * P)
+            if quarter % 2 == 0:
+                nc.vector.tensor_scalar(z_bf[:, cols, t], target[:, cols], gain, None, ALU.mult)
+            else:
+                nc.scalar.activation(z_bf[:, cols, t], target[:, cols], COPY, scale=gain)
+
+        for half in range(2):
+            cols = slice(half * HALF, (half + 1) * HALF)
+            z_words = keep.tile([P, HALF], U32, name="z_words%d" % half, align_bytes=64)
+            z_scales = keep.tile([P, HALF], U8, name="z_scales%d" % half, align_bytes=64)
+            nc.vector.quantize_mx(
+                out=z_words[:].bitcast(FP8X4),
+                scales=z_scales[:],
+                in_=z_bf[:, cols, :].rearrange("p s t -> p (s t)"),
+            )
+            for c in range(C // P):
+                rows = slice(c * P, (c + 1) * P)
+                acc = psum.tile([P, HALF], F32, name="acc")
+                nc.tensor.matmul_mx(
+                    out=acc[:],
+                    lhsT=cand_words[:, rows].bitcast(FP8X4),
+                    lhsT_scale=cand_scales[:, rows],
+                    rhs=z_words[:].bitcast(FP8X4),
+                    rhs_scale=z_scales[:],
+                    start=True,
+                    stop=True,
+                )
+                res = keep.tile([P, HALF], F32, name="res%d_%d" % (half, c))
+                if c % 2 == 0:
+                    nc.scalar.activation(res[:], acc[:], COPY, scale=OUT_SCALE)
+                else:
+                    nc.vector.tensor_scalar(res[:], acc[:], OUT_SCALE, None, ALU.mult)
+                nc.sync.dma_start(out[rows, cols], res[:])

@@ -38,17 +38,17 @@ def tile_picked_bitonic2_none_p_kernel(tc, x_words, x_scales, w1, gs, offs, la, 
         nc.vector.memset(table_scales[:].bitcast(I32), 0)
 
         w_rows = w1.rearrange("(p j) c -> p j c", j=PACK)
-        w_raw = [keep.tile([P, PACK, HALF], F32, name="w_raw%d" % i) for i in range(2)]
-        nc.sync.dma_start(w_raw[0][:], w_rows[:, :, 0:HALF])
+        w_raw = [keep.tile([P, 2, H], F32, name="w_raw%d" % i) for i in range(2)]
+        offs_t = load_list("offs_t", offs)
+        cand_t = load_list("cand_t", cand)
+        nc.sync.dma_start(w_raw[0][:], w_rows[:, 0:2, :])
         for q in range(4):
             nc.sync.dma_start(
                 table_scales[32 * q : 32 * q + 4, :].bitcast(I32),
                 x_scales[0, 4 * q : 4 * q + 4, :].bitcast(I32),
             )
-        nc.sync.dma_start(w_raw[1][:], w_rows[:, :, HALF : 2 * HALF])
-        offs_t = load_list("offs_t", offs)
         nc.sync.dma_start(table_words[:], x_words[0].rearrange("p n t -> p (n t)").bitcast(I32))
-        cand_t = load_list("cand_t", cand)
+        nc.sync.dma_start(w_raw[1][:], w_rows[:, 2:4, :])
         la_t = load_list("la_t", la)
         lb_t = load_list("lb_t", lb)
         ma_t = load_list("ma_t", ma)
@@ -59,44 +59,52 @@ def tile_picked_bitonic2_none_p_kernel(tc, x_words, x_scales, w1, gs, offs, la, 
         tok_scales = keep.tile([P, S], U8, name="tok_scales", align_bytes=64)
         cand_scales = keep.tile([P, C], U8, name="cand_scales", align_bytes=64)
         tok_words = keep.tile([P, S], U32, name="tok_words", align_bytes=64)
-        cand_words = keep.tile([P, C], U32, name="cand_words", align_bytes=64)
         nc.vector.tensor_copy(tok_scales[:], table_scales[:].indirect(offs_t[:]))
         nc.vector.tensor_copy(cand_scales[:], table_scales[:].indirect(cand_t[:]))
-
-        w_bf = keep.tile([P, PACK, P, PACK], BF16, name="w_bf", align_bytes=64)
-        per = HALF // PACK
-        for i in range(2):
-            nc.scalar.copy(
-                w_bf[:, :, i * per : (i + 1) * per, :].rearrange("p t m j -> p m t j"),
-                w_raw[i][:].rearrange("p j (m t) -> p m t j", t=PACK),
-            )
-        w_words = keep.tile([P, H], U32, name="w_words", align_bytes=64)
-        w_scales = keep.tile([P, H], U8, name="w_scales", align_bytes=64)
-        nc.vector.quantize_mx(
-            out=w_words[:].bitcast(FP8X4),
-            scales=w_scales[:],
-            in_=w_bf[:].rearrange("p t m j -> p (t m j)"),
-        )
-
         nc.vector.tensor_copy(tok_words[:], table_words[:].bitcast(U32).indirect(offs_t[:]))
-        nc.vector.tensor_copy(cand_words[:], table_words[:].bitcast(U32).indirect(cand_t[:]))
 
         order = (2, 0, 1, 3)
+        w_bf = {}
+
+        def cast_w(t, i, copy):
+            copy(
+                w_bf[t][:, :, 2 * i : 2 * i + 2],
+                w_raw[i][:].rearrange("p j (m t) -> p t m j", t=PACK)[:, t],
+            )
+
+        for n, t in enumerate(order[:3]):
+            w_bf[t] = keep.tile([P, P, PACK], BF16, name="w_bf%d" % t, tag="w_bf%d" % n, align_bytes=64)
+            cast_w(t, 0, nc.scalar.copy)
         y = {}
         for t in order:
-            acc = psum.tile([P, S], F32, name="acc")
-            cols = slice(t * P, (t + 1) * P)
-            nc.tensor.matmul_mx(
-                out=acc[:],
-                lhsT=w_words[:, cols].bitcast(FP8X4),
-                lhsT_scale=w_scales[:, cols],
-                rhs=tok_words[:].bitcast(FP8X4),
-                rhs_scale=tok_scales[:],
-                start=True,
-                stop=True,
+            if t == order[3]:
+                w_bf[t] = keep.tile([P, P, PACK], BF16, name="w_bf%d" % t, tag="w_bf1", align_bytes=64)
+                cast_w(t, 0, nc.scalar.copy)
+            cast_w(t, 1, nc.vector.tensor_copy if t == order[0] else nc.scalar.copy)
+            w_words = keep.tile([P, P], U32, name="w_words%d" % t, align_bytes=64)
+            w_scales = keep.tile([P, P], U8, name="w_scales%d" % t, align_bytes=64)
+            nc.vector.quantize_mx(
+                out=w_words[:].bitcast(FP8X4),
+                scales=w_scales[:],
+                in_=w_bf[t][:].rearrange("p m j -> p (m j)"),
             )
+            if t == order[0]:
+                cand_words = keep.tile([P, C], U32, name="cand_words", tag="w_bf0", align_bytes=64)
+                nc.vector.tensor_copy(cand_words[:], table_words[:].bitcast(U32).indirect(cand_t[:]))
             y[t] = keep.tile([P, S], F32, name="y%d" % t)
-            nc.scalar.copy(y[t][:], acc[:])
+            for half in range(2):
+                cols = slice(half * HALF, (half + 1) * HALF)
+                acc = psum.tile([P, HALF], F32, name="acc")
+                nc.tensor.matmul_mx(
+                    out=acc[:],
+                    lhsT=w_words[:].bitcast(FP8X4),
+                    lhsT_scale=w_scales[:],
+                    rhs=tok_words[:, cols].bitcast(FP8X4),
+                    rhs_scale=tok_scales[:, cols],
+                    start=True,
+                    stop=True,
+                )
+                nc.scalar.copy(y[t][:, cols], acc[:])
 
         h = {t: keep.tile([P, S], F32, name="h%d" % t) for t in order}
         steps = [(0, t) for t in order] + [(1, t) for t in order]
@@ -110,9 +118,14 @@ def tile_picked_bitonic2_none_p_kernel(tc, x_words, x_scales, w1, gs, offs, la, 
             nc.vector.tensor_copy(got[:], window[:].indirect(lists[stage][side][:]))
             return got
 
+        def put(step, side, target, values):
+            nc.vector.tensor_copy(target[:].indirect(lists[step[0]][side][:]), values[:])
+
         a = fetch(steps[0], 0)
         b = fetch(steps[0], 1)
-        for n, (stage, t) in enumerate(steps):
+        pending = None
+        for n, step in enumerate(steps):
+            stage, t = step
             more = n + 1 < len(steps)
             lo = ring.tile([P, V], F32, name="lo")
             hi = ring.tile([P, V], F32, name="hi")
@@ -124,45 +137,52 @@ def tile_picked_bitonic2_none_p_kernel(tc, x_words, x_scales, w1, gs, offs, la, 
                 target = ring.tile([P, S], F32, name="h3")
             if more:
                 a = fetch(steps[n + 1], 0)
-            nc.vector.tensor_copy(target[:].indirect(lists[stage][0][:]), lo[:])
+            put(step, 0, target, lo)
             if more:
                 b = fetch(steps[n + 1], 1)
-            nc.vector.tensor_copy(target[:].indirect(lists[stage][1][:]), hi[:])
-            if stage == 1 and more:
-                nc.scalar.activation(z_bf[:, :, t], target[:], COPY, scale=gains[:, t : t + 1])
+            if pending is not None:
+                (p_stage, p_t), p_target, p_hi = pending
+                put(pending[0], 1, p_target, p_hi)
+                if p_stage == 1:
+                    nc.scalar.activation(z_bf[:, :, p_t], p_target[:], COPY, scale=gains[:, p_t : p_t + 1])
+            pending = (step, target, hi)
+        put(step, 1, target, hi)
 
         gain = gains[:, t : t + 1]
-        for quarter in range(4):
-            cols = slice(quarter * P, (quarter + 1) * P)
-            if quarter % 2 == 0:
-                nc.vector.tensor_scalar(z_bf[:, cols, t], target[:, cols], gain, None, ALU.mult)
-            else:
-                nc.scalar.activation(z_bf[:, cols, t], target[:, cols], COPY, scale=gain)
+        chunks = (slice(0, P), slice(P, HALF), slice(HALF, S))
+        for cols in chunks[:2]:
+            nc.vector.tensor_scalar(z_bf[:, cols, t], target[:, cols], gain, None, ALU.mult)
+        nc.scalar.activation(z_bf[:, chunks[2], t], target[:, chunks[2]], COPY, scale=gain)
 
-        for half in range(2):
-            cols = slice(half * HALF, (half + 1) * HALF)
-            z_words = keep.tile([P, HALF], U32, name="z_words%d" % half, align_bytes=64)
-            z_scales = keep.tile([P, HALF], U8, name="z_scales%d" % half, align_bytes=64)
+        res = [[keep.tile([P, HALF], F32, name="res%d_%d" % (half, c)) for c in range(C // P)] for half in range(2)]
+        z_mx = []
+        for n, cols in enumerate(chunks):
+            width = cols.stop - cols.start
+            z_words = keep.tile([P, width], U32, name="z_words%d" % n, align_bytes=64)
+            z_scales = keep.tile([P, width], U8, name="z_scales%d" % n, align_bytes=64)
             nc.vector.quantize_mx(
                 out=z_words[:].bitcast(FP8X4),
                 scales=z_scales[:],
                 in_=z_bf[:, cols, :].rearrange("p s t -> p (s t)"),
             )
+            z_mx.append((cols, z_words, z_scales))
+        for half, parts in enumerate((z_mx[:2], z_mx[2:])):
             for c in range(C // P):
                 rows = slice(c * P, (c + 1) * P)
-                acc = psum.tile([P, HALF], F32, name="acc")
-                nc.tensor.matmul_mx(
-                    out=acc[:],
-                    lhsT=cand_words[:, rows].bitcast(FP8X4),
-                    lhsT_scale=cand_scales[:, rows],
-                    rhs=z_words[:].bitcast(FP8X4),
-                    rhs_scale=z_scales[:],
-                    start=True,
-                    stop=True,
-                )
-                res = keep.tile([P, HALF], F32, name="res%d_%d" % (half, c))
-                if c % 2 == 0:
-                    nc.scalar.activation(res[:], acc[:], COPY, scale=OUT_SCALE)
-                else:
-                    nc.vector.tensor_scalar(res[:], acc[:], OUT_SCALE, None, ALU.mult)
-                nc.sync.dma_start(out[rows, cols], res[:])
+                for cols, z_words, z_scales in parts:
+                    acc = psum.tile([P, cols.stop - cols.start], F32, name="acc")
+                    nc.tensor.matmul_mx(
+                        out=acc[:],
+                        lhsT=cand_words[:, rows].bitcast(FP8X4),
+                        lhsT_scale=cand_scales[:, rows],
+                        rhs=z_words[:].bitcast(FP8X4),
+                        rhs_scale=z_scales[:],
+                        start=True,
+                        stop=True,
+                    )
+                    piece = res[half][c][:, cols.start - half * HALF : cols.stop - half * HALF]
+                    if c % 2 == 0:
+                        nc.scalar.activation(piece, acc[:], COPY, scale=OUT_SCALE)
+                    else:
+                        nc.vector.tensor_scalar(piece, acc[:], OUT_SCALE, None, ALU.mult)
+                nc.sync.dma_start(out[rows, half * HALF : (half + 1) * HALF], res[half][c][:])

@@ -38,17 +38,17 @@ def tile_picked_bitonic2_none_p_kernel(tc, x_words, x_scales, w1, gs, offs, la, 
         nc.vector.memset(table_scales[:].bitcast(I32), 0)
 
         w_rows = w1.rearrange("(p j) c -> p j c", j=PACK)
-        w_raw = [keep.tile([P, 2, H], F32, name="w_raw%d" % i) for i in range(2)]
+        w_raw = [keep.tile([P, PACK, HALF], F32, name="w_raw%d" % i) for i in range(2)]
         offs_t = load_list("offs_t", offs)
+        nc.sync.dma_start(w_raw[0][:], w_rows[:, :, 0:HALF])
         cand_t = load_list("cand_t", cand)
-        nc.sync.dma_start(w_raw[0][:], w_rows[:, 0:2, :])
         for q in range(4):
             nc.sync.dma_start(
                 table_scales[32 * q : 32 * q + 4, :].bitcast(I32),
                 x_scales[0, 4 * q : 4 * q + 4, :].bitcast(I32),
             )
+        nc.sync.dma_start(w_raw[1][:], w_rows[:, :, HALF:H])
         nc.sync.dma_start(table_words[:], x_words[0].rearrange("p n t -> p (n t)").bitcast(I32))
-        nc.sync.dma_start(w_raw[1][:], w_rows[:, 2:4, :])
         la_t = load_list("la_t", la)
         lb_t = load_list("lb_t", lb)
         ma_t = load_list("ma_t", ma)
@@ -58,48 +58,55 @@ def tile_picked_bitonic2_none_p_kernel(tc, x_words, x_scales, w1, gs, offs, la, 
 
         tok_scales = keep.tile([P, S], U8, name="tok_scales", align_bytes=64)
         cand_scales = keep.tile([P, C], U8, name="cand_scales", align_bytes=64)
-        tok_words = keep.tile([P, S], U32, name="tok_words", align_bytes=64)
         nc.vector.tensor_copy(tok_scales[:], table_scales[:].indirect(offs_t[:]))
         nc.vector.tensor_copy(cand_scales[:], table_scales[:].indirect(cand_t[:]))
-        nc.vector.tensor_copy(tok_words[:], table_words[:].bitcast(U32).indirect(offs_t[:]))
 
         order = (2, 0, 1, 3)
-        w_bf = {}
+        per = HALF // PACK
+        w_bf = {u: keep.tile([P, 2, P, PACK], BF16, name="w_bf%d" % u, tag="w_bf%d" % u, align_bytes=64) for u in (1, 0)}
+        for i in range(2):
+            for u in (1, 0):
+                nc.scalar.copy(
+                    w_bf[u][:, :, i * per : (i + 1) * per, :].rearrange("p t m j -> p m t j"),
+                    w_raw[i][:].rearrange("p j (m t) -> p m t j", t=PACK)[:, :, 2 * u : 2 * u + 2, :],
+                )
 
-        def cast_w(t, i, copy):
-            copy(
-                w_bf[t][:, :, 2 * i : 2 * i + 2],
-                w_raw[i][:].rearrange("p j (m t) -> p t m j", t=PACK)[:, t],
+        def quantize_w(u):
+            words = keep.tile([P, HALF], U32, name="w_words%d" % u, align_bytes=64)
+            scales = keep.tile([P, HALF], U8, name="w_scales%d" % u, align_bytes=64)
+            nc.vector.quantize_mx(
+                out=words[:].bitcast(FP8X4),
+                scales=scales[:],
+                in_=w_bf[u][:].rearrange("p t m j -> p (t m j)"),
             )
+            return words, scales
 
-        for n, t in enumerate(order[:3]):
-            w_bf[t] = keep.tile([P, P, PACK], BF16, name="w_bf%d" % t, tag="w_bf%d" % n, align_bytes=64)
-            cast_w(t, 0, nc.scalar.copy)
+        def gather_words(name, tag, entries):
+            words = keep.tile([P, 16 * entries.shape[1]], U32, name=name, tag=tag, align_bytes=64)
+            nc.vector.tensor_copy(words[:], table_words[:].bitcast(U32).indirect(entries))
+            return words
+
+        w_mx = {1: quantize_w(1)}
+        tok_words = [
+            gather_words("tok_words0", "w_bf1", offs_t[:, 0 : HALF // 16]),
+            gather_words("tok_words1", "tok_words1", offs_t[:, HALF // 16 : S // 16]),
+        ]
+        w_mx[0] = quantize_w(0)
+        cand_words = gather_words("cand_words", "w_bf0", cand_t[:])
+
         y = {}
         for t in order:
-            if t == order[3]:
-                w_bf[t] = keep.tile([P, P, PACK], BF16, name="w_bf%d" % t, tag="w_bf1", align_bytes=64)
-                cast_w(t, 0, nc.scalar.copy)
-            cast_w(t, 1, nc.vector.tensor_copy if t == order[0] else nc.scalar.copy)
-            w_words = keep.tile([P, P], U32, name="w_words%d" % t, align_bytes=64)
-            w_scales = keep.tile([P, P], U8, name="w_scales%d" % t, align_bytes=64)
-            nc.vector.quantize_mx(
-                out=w_words[:].bitcast(FP8X4),
-                scales=w_scales[:],
-                in_=w_bf[t][:].rearrange("p m j -> p (m j)"),
-            )
-            if t == order[0]:
-                cand_words = keep.tile([P, C], U32, name="cand_words", tag="w_bf0", align_bytes=64)
-                nc.vector.tensor_copy(cand_words[:], table_words[:].bitcast(U32).indirect(cand_t[:]))
+            w_words, w_scales = w_mx[t // 2]
+            w_cols = slice((t % 2) * P, (t % 2 + 1) * P)
             y[t] = keep.tile([P, S], F32, name="y%d" % t)
             for half in range(2):
                 cols = slice(half * HALF, (half + 1) * HALF)
                 acc = psum.tile([P, HALF], F32, name="acc")
                 nc.tensor.matmul_mx(
                     out=acc[:],
-                    lhsT=w_words[:].bitcast(FP8X4),
-                    lhsT_scale=w_scales[:],
-                    rhs=tok_words[:, cols].bitcast(FP8X4),
+                    lhsT=w_words[:, w_cols].bitcast(FP8X4),
+                    lhsT_scale=w_scales[:, w_cols],
+                    rhs=tok_words[half][:].bitcast(FP8X4),
                     rhs_scale=tok_scales[:, cols],
                     start=True,
                     stop=True,
@@ -107,46 +114,41 @@ def tile_picked_bitonic2_none_p_kernel(tc, x_words, x_scales, w1, gs, offs, la, 
                 nc.scalar.copy(y[t][:, cols], acc[:])
 
         h = {t: keep.tile([P, S], F32, name="h%d" % t) for t in order}
-        steps = [(0, t) for t in order] + [(1, t) for t in order]
+        pairs = (order[:2], order[2:])
+        steps = [(stage, pair) for stage in range(2) for pair in pairs]
         lists = ((la_t, lb_t), (ma_t, mb_t))
         z_bf = keep.tile([P, S, PACK], BF16, name="z_bf", align_bytes=64)
 
-        def fetch(step, side):
-            stage, t = step
-            window = y[t] if stage == 0 else h[t]
-            got = ring.tile([P, V], F32, name="got%d" % side)
-            nc.vector.tensor_copy(got[:], window[:].indirect(lists[stage][side][:]))
-            return got
+        def fetches(step):
+            stage, pair = step
+            got = [ring.tile([P, 2, V], F32, name="got%d" % side) for side in range(2)]
+            calls = [
+                (got[side][:, i, :], (y[t] if stage == 0 else h[t])[:].indirect(lists[stage][side][:]))
+                for i, t in enumerate(pair)
+                for side in range(2)
+            ]
+            return got, calls
 
-        def put(step, side, target, values):
-            nc.vector.tensor_copy(target[:].indirect(lists[step[0]][side][:]), values[:])
-
-        a = fetch(steps[0], 0)
-        b = fetch(steps[0], 1)
-        pending = None
-        for n, step in enumerate(steps):
-            stage, t = step
-            more = n + 1 < len(steps)
-            lo = ring.tile([P, V], F32, name="lo")
-            hi = ring.tile([P, V], F32, name="hi")
+        (a, b), calls = fetches(steps[0])
+        for dst, src in calls:
+            nc.vector.tensor_copy(dst, src)
+        for n, (stage, pair) in enumerate(steps):
+            lo = ring.tile([P, 2, V], F32, name="lo")
+            hi = ring.tile([P, 2, V], F32, name="hi")
             nc.vector.tensor_tensor(lo[:], a[:], b[:], ALU.min)
             nc.vector.tensor_tensor(hi[:], a[:], b[:], ALU.max)
-            if stage == 0:
-                target = h[t]
-            else:
-                target = ring.tile([P, S], F32, name="h3")
-            if more:
-                a = fetch(steps[n + 1], 0)
-            put(step, 0, target, lo)
-            if more:
-                b = fetch(steps[n + 1], 1)
-            if pending is not None:
-                (p_stage, p_t), p_target, p_hi = pending
-                put(pending[0], 1, p_target, p_hi)
-                if p_stage == 1:
-                    nc.scalar.activation(z_bf[:, :, p_t], p_target[:], COPY, scale=gains[:, p_t : p_t + 1])
-            pending = (step, target, hi)
-        put(step, 1, target, hi)
+            calls = []
+            if n + 1 < len(steps):
+                (a, b), calls = fetches(steps[n + 1])
+            targets = [h[t] if stage == 0 else ring.tile([P, S], F32, name="h3") for t in pair]
+            for side, values in enumerate((lo, hi)):
+                for i, t in enumerate(pair):
+                    if calls:
+                        nc.vector.tensor_copy(*calls[2 * side + i])
+                    nc.vector.tensor_copy(targets[i][:].indirect(lists[stage][side][:]), values[:, i, :])
+                    if stage == 1 and side == 1 and t != order[-1]:
+                        nc.scalar.activation(z_bf[:, :, t], targets[i][:], COPY, scale=gains[:, t : t + 1])
+        target = targets[-1]
 
         gain = gains[:, t : t + 1]
         chunks = (slice(0, P), slice(P, HALF), slice(HALF, S))
@@ -166,6 +168,7 @@ def tile_picked_bitonic2_none_p_kernel(tc, x_words, x_scales, w1, gs, offs, la, 
                 in_=z_bf[:, cols, :].rearrange("p s t -> p (s t)"),
             )
             z_mx.append((cols, z_words, z_scales))
+        passes = 0
         for half, parts in enumerate((z_mx[:2], z_mx[2:])):
             for c in range(C // P):
                 rows = slice(c * P, (c + 1) * P)
@@ -181,7 +184,8 @@ def tile_picked_bitonic2_none_p_kernel(tc, x_words, x_scales, w1, gs, offs, la, 
                         stop=True,
                     )
                     piece = res[half][c][:, cols.start - half * HALF : cols.stop - half * HALF]
-                    if c % 2 == 0:
+                    passes = passes + 1
+                    if passes % 2 == 1:
                         nc.scalar.activation(piece, acc[:], COPY, scale=OUT_SCALE)
                     else:
                         nc.vector.tensor_scalar(piece, acc[:], OUT_SCALE, None, ALU.mult)

from contextlib import ExitStack

import concourse.mybir as mybir

K, T, S, V, H, C = 512, 2048, 512, 256, 512, 512
FLOPS = 2 * K * H * S + 2 * H * C * S

F32 = mybir.dt.float32
BF16 = mybir.dt.bfloat16
I32 = mybir.dt.int32
U32 = mybir.dt.uint32
U16 = mybir.dt.uint16
U8 = mybir.dt.uint8
FP8X4 = mybir.dt.float8_e4m3fn_x4
ALU = mybir.AluOpType
COPY = mybir.ActivationFunctionType.Copy

P = 128
PACK = 4
HALF = 256
OUT_SCALE = 0.0625


def tile_picked_bitonic2_none_p_kernel(tc, x_words, x_scales, w1, gs, offs, la, lb, ma, mb, cand, out):
    nc = tc.nc
    with ExitStack() as ctx:
        keep = ctx.enter_context(tc.tile_pool(name="keep", bufs=1))
        ring = ctx.enter_context(tc.tile_pool(name="ring", bufs=3))
        psum = ctx.enter_context(tc.psum_pool(name="psum", bufs=8))

        def load_list(name, src):
            tile = keep.tile(list(src.shape), U16, name=name)
            nc.sync.dma_start(tile[:], src)
            return tile

        table_words = keep.tile([P, T], I32, name="table_words", align_bytes=64)
        table_scales = keep.tile([P, T], U8, name="table_scales", align_bytes=64)
        nc.vector.memset(table_scales[:].bitcast(I32), 0)

        w_rows = w1.rearrange("(p j) c -> p j c", j=PACK)
        w_raw = [keep.tile([P, PACK, HALF], F32, name="w_raw%d" % i) for i in range(2)]
        offs_t = load_list("offs_t", offs)
        nc.sync.dma_start(w_raw[0][:], w_rows[:, :, 0:HALF])
        cand_t = load_list("cand_t", cand)
        for q in range(4):
            nc.sync.dma_start(
                table_scales[32 * q : 32 * q + 4, :].bitcast(I32),
                x_scales[0, 4 * q : 4 * q + 4, :].bitcast(I32),
            )
        nc.sync.dma_start(w_raw[1][:], w_rows[:, :, HALF:H])
        nc.sync.dma_start(table_words[:], x_words[0].rearrange("p n t -> p (n t)").bitcast(I32))
        la_t = load_list("la_t", la)
        lb_t = load_list("lb_t", lb)
        ma_t = load_list("ma_t", ma)
        mb_t = load_list("mb_t", mb)
        gains = keep.tile([P, PACK], F32, name="gains")
        nc.sync.dma_start(gains[:], gs.rearrange("(p t) o -> p (t o)", t=PACK))

        tok_scales = keep.tile([P, S], U8, name="tok_scales", align_bytes=64)
        cand_scales = keep.tile([P, C], U8, name="cand_scales", align_bytes=64)
        nc.vector.tensor_copy(tok_scales[:], table_scales[:].indirect(offs_t[:]))
        nc.vector.tensor_copy(cand_scales[:], table_scales[:].indirect(cand_t[:]))

        order = (2, 0, 1, 3)
        per = HALF // PACK
        w_bf = {u: keep.tile([P, 2, P, PACK], BF16, name="w_bf%d" % u, tag="w_bf%d" % u, align_bytes=64) for u in (1, 0)}
        for i in range(2):
            for u in (1, 0):
                nc.scalar.copy(
                    w_bf[u][:, :, i * per : (i + 1) * per, :].rearrange("p t m j -> p m t j"),
                    w_raw[i][:].rearrange("p j (m t) -> p m t j", t=PACK)[:, :, 2 * u : 2 * u + 2, :],
                )

        def quantize_w(u):
            words = keep.tile([P, HALF], U32, name="w_words%d" % u, align_bytes=64)
            scales = keep.tile([P, HALF], U8, name="w_scales%d" % u, align_bytes=64)
            nc.vector.quantize_mx(
                out=words[:].bitcast(FP8X4),
                scales=scales[:],
                in_=w_bf[u][:].rearrange("p t m j -> p (t m j)"),
            )
            return words, scales

        def gather_words(name, tag, entries):
            words = keep.tile([P, 16 * entries.shape[1]], U32, name=name, tag=tag, align_bytes=64)
            nc.vector.tensor_copy(words[:], table_words[:].bitcast(U32).indirect(entries))
            return words

        w_mx = {1: quantize_w(1)}
        tok_words = [
            gather_words("tok_words0", "w_bf1", offs_t[:, 0 : HALF // 16]),
            gather_words("tok_words1", "tok_words1", offs_t[:, HALF // 16 : S // 16]),
        ]
        w_mx[0] = quantize_w(0)
        cand_words = gather_words("cand_words", "w_bf0", cand_t[:])

        y = {}
        for t in order:
            w_words, w_scales = w_mx[t // 2]
            w_cols = slice((t % 2) * P, (t % 2 + 1) * P)
            y[t] = keep.tile([P, S], F32, name="y%d" % t)
            for half in range(2):
                cols = slice(half * HALF, (half + 1) * HALF)
                acc = psum.tile([P, HALF], F32, name="acc")
                nc.tensor.matmul_mx(
                    out=acc[:],
                    lhsT=w_words[:, w_cols].bitcast(FP8X4),
                    lhsT_scale=w_scales[:, w_cols],
                    rhs=tok_words[half][:].bitcast(FP8X4),
                    rhs_scale=tok_scales[:, cols],
                    start=True,
                    stop=True,
                )
                nc.scalar.copy(y[t][:, cols], acc[:])

        h = {t: keep.tile([P, S], F32, name="h%d" % t) for t in order}
        pairs = (order[:2], order[2:])
        steps = [(stage, pair) for stage in range(2) for pair in pairs]
        lists = ((la_t, lb_t), (ma_t, mb_t))
        z_bf = keep.tile([P, S, PACK], BF16, name="z_bf", align_bytes=64)

        def fetches(step):
            stage, pair = step
            got = [ring.tile([P, 2, V], F32, name="got%d" % side) for side in range(2)]
            calls = [
                (got[side][:, i, :], (y[t] if stage == 0 else h[t])[:].indirect(lists[stage][side][:]))
                for i, t in enumerate(pair)
                for side in range(2)
            ]
            return got, calls

        (a, b), calls = fetches(steps[0])
        for dst, src in calls:
            nc.vector.tensor_copy(dst, src)
        for n, (stage, pair) in enumerate(steps):
            lo = ring.tile([P, 2, V], F32, name="lo")
            hi = ring.tile([P, 2, V], F32, name="hi")
            nc.vector.tensor_tensor(lo[:], a[:], b[:], ALU.min)
            nc.vector.tensor_tensor(hi[:], a[:], b[:], ALU.max)
            calls = []
            if n + 1 < len(steps):
                (a, b), calls = fetches(steps[n + 1])
            targets = [h[t] if stage == 0 else ring.tile([P, S], F32, name="h3") for t in pair]
            for side, values in enumerate((lo, hi)):
                for i, t in enumerate(pair):
                    if calls:
                        nc.vector.tensor_copy(*calls[2 * side + i])
                    nc.vector.tensor_copy(targets[i][:].indirect(lists[stage][side][:]), values[:, i, :])
                    if stage == 1 and side == 1 and t != order[-1]:
                        nc.scalar.activation(z_bf[:, :, t], targets[i][:], COPY, scale=gains[:, t : t + 1])
        target = targets[-1]

        gain = gains[:, t : t + 1]
        chunks = (slice(0, P), slice(P, HALF), slice(HALF, S))
        for cols in chunks[:2]:
            nc.vector.tensor_scalar(z_bf[:, cols, t], target[:, cols], gain, None, ALU.mult)
        nc.scalar.activation(z_bf[:, chunks[2], t], target[:, chunks[2]], COPY, scale=gain)

        res = [[keep.tile([P, HALF], F32, name="res%d_%d" % (half, c)) for c in range(C // P)] for half in range(2)]
        z_mx = []
        for n, cols in enumerate(chunks):
            width = cols.stop - cols.start
            z_words = keep.tile([P, width], U32, name="z_words%d" % n, align_bytes=64)
            z_scales = keep.tile([P, width], U8, name="z_scales%d" % n, align_bytes=64)
            nc.vector.quantize_mx(
                out=z_words[:].bitcast(FP8X4),
                scales=z_scales[:],
                in_=z_bf[:, cols, :].rearrange("p s t -> p (s t)"),
            )
            z_mx.append((cols, z_words, z_scales))
        passes = 0
        for half, parts in enumerate((z_mx[:2], z_mx[2:])):
            for c in range(C // P):
                rows = slice(c * P, (c + 1) * P)
                for cols, z_words, z_scales in parts:
                    acc = psum.tile([P, cols.stop - cols.start], F32, name="acc")
                    nc.tensor.matmul_mx(
                        out=acc[:],
                        lhsT=cand_words[:, rows].bitcast(FP8X4),
                        lhsT_scale=cand_scales[:, rows],
                        rhs=z_words[:].bitcast(FP8X4),
                        rhs_scale=z_scales[:],
                        start=True,
                        stop=True,
                    )
                    piece = res[half][c][:, cols.start - half * HALF : cols.stop - half * HALF]
                    passes = passes + 1
                    if passes % 2 == 1:
                        nc.scalar.activation(piece, acc[:], COPY, scale=OUT_SCALE)
                    else:
                        nc.vector.tensor_scalar(piece, acc[:], OUT_SCALE, None, ALU.mult)
                nc.sync.dma_start(out[rows, half * HALF : (half + 1) * HALF], res[half][c][:])
